import numpy as np, ml_dtypes
CORES = [51,54,179,182]
N = 4
import mx_ref
BF = ml_dtypes.bfloat16
def entries(a):
    return np.ascontiguousarray(a.T).reshape(-1)
def table(e):
    return np.ascontiguousarray(np.reshape(e, (-1, 16)).T).astype(np.int32)
def gpick(z, e):
    return np.concatenate([z[16 * g:16 * g + 16][:, e[g]] for g in range(8)])
def tile(rs):
    return np.stack(rs, axis=2).reshape(128, -1).astype(BF)
def cut(t, i, w=512):
    return t[:, w * i:w * i + w]
def f(rng, *shape):
    return mx_ref.flush((rng.standard_normal(shape, dtype=np.float32) * np.exp2(rng.integers(-2, 3, shape[:-1] + (1,)))).astype(BF))
def wide(rng, *shape, cols=0):
    v = rng.standard_normal(shape, dtype=np.float32) * np.exp2(rng.integers(-12, 13, shape)).astype(np.float32)
    if cols: v *= np.repeat(np.exp2(rng.integers(-cols, cols + 1, shape[:-2] + (1, shape[-1] // 4))) * (rng.random(shape[:-2] + (1, shape[-1] // 4)) > 0.0625), 4, axis=-1).astype(np.float32)
    return mx_ref.flush(v.astype(BF))
TQ, O = 256, 1
def lay(k, q):
    return {"kp": np.repeat(k, 16, axis=1).astype(np.int32), "qp": np.stack([table(e) for e in q])}
def setup_inputs(rng):
    d = {"qx": f(rng, N, 128, 4 * TQ), "ky": f(rng, N, 128, 2048), "rt": np.repeat(f(rng, 1, 128, 1024), N, axis=0), "vv": f(rng, N, 128, 512 * O)}
    a = rng.integers(0, 3585)
    k = a + rng.integers(0, 512, (N, 8, 4))
    q = np.where(rng.random((N, TQ)) < 0.25, rng.integers(0, 4096, (N, TQ)), a + rng.integers(0, 512, (N, TQ)))
    return {**d, **lay(k, q)}
def setup_inputs_far(rng):
    d = setup_inputs(rng)
    k = rng.integers(1500, 2501, (N, 32)); q = np.zeros((N, TQ), int); a = int(rng.integers(0, 2))
    for r in range(N):
        k[r, rng.permutation(32)[:2]] = [1500, 2500]
        lo, hi = (2628, 4095) if (r + a) % 2 else (0, 1371)
        q[r] = rng.integers(lo, hi + 1, TQ)
        q[r, rng.permutation(TQ)[:2]] = [lo, hi]
    return {**d, **lay(k.reshape(N, 8, 4), q)}
def setup_inputs_same(rng):
    d = setup_inputs(rng); a = int(rng.integers(0, 4096))
    return {**d, **lay(np.full((N, 8, 4), a), np.full((N, TQ), a))}
def setup_inputs_descending(rng):
    d = setup_inputs(rng); a = rng.integers(0, 3585)
    q = np.stack([a + np.sort(rng.permutation(512)[:TQ])[::-1] for r in range(N)])
    k = np.stack([a + 16 * rng.permutation(32) + rng.integers(0, 16, 32) for r in range(N)])
    return {**d, **lay(k.reshape(N, 8, 4), q)}
def setup_inputs_near(rng):
    d = setup_inputs(rng); a = rng.integers(2049, 3968)
    q = np.stack([a + rng.permutation(TQ) % 128 for r in range(N)])
    k = np.stack([a + rng.permutation(np.concatenate([[0, 128], 1 + rng.permutation(127)[:30]])) for r in range(N)])
    return {**d, **lay(k.reshape(N, 8, 4), q)}
def setup_inputs_spread(rng):
    d = setup_inputs(rng); d["qx"] = wide(rng, N, 128, 4 * TQ, cols=4); return d
def check_inputs(d):
    b = []
    for r in range(N):
        k, q = d["kp"][r], entries(d["qp"][r])
        if d["rt"][r].tobytes() != d["rt"][0].tobytes(): b.append("rt")
        if k.min() < 0 or k.max() > 4095 or (k != np.repeat(k[::16], 16, axis=0)).any(): b.append("kp")
        if q.min() < 0 or q.max() > 4095: b.append("qp")
    return b
def reference(qx, ky, rt, vv, kp, qp):
    y = np.zeros((N, 128, O * TQ), np.float32)
    X = [mx_ref.quantize(qx[r]) for r in range(N)]
    for s in range(N):
        K = [mx_ref.quantize(np.ascontiguousarray(cut(ky[s], b))) for b in range(4)]
        V = [mx_ref.quantize(np.ascontiguousarray(cut(vv[s], o))) for o in range(O)]
        R = mx_ref.quantize(rt[s])
        P = [mx_ref.matmul(K[b], R) for b in range(4)]
        for r in range(N):
            A = []
            for b in range(4):
                c = np.clip(entries(qp[r])[None, :] - kp[s][::16, b][:, None], -128, 127) + 128
                A.append(np.maximum(mx_ref.matmul(K[b], X[r]) + gpick(P[b], c), np.float32(0)) * np.float32(0.03125))
            A = mx_ref.quantize(tile(A))
            for o in range(O): y[r][:, TQ * o:TQ * o + TQ] += mx_ref.matmul(V[o], A)
    return {"y": y}

@@ -1,0 +1,255 @@
+from concourse.bass import DstId, RemoteDMATransfer
+from concourse.mybir import dt, AluOpType, ActivationFunctionType
+
+CODES = "float8_e4m3fn_x4"
+SCRATCH = {
+    "ky_b": ("sbuf", [128, 2048], "bfloat16"),
+    "qx_b": ("sbuf", [128, 1024], "bfloat16"),
+    "rt_b": ("sbuf", [128, 1024], "bfloat16"),
+    "vv_b": ("sbuf", [128, 512], "bfloat16"),
+    "pz": ("sbuf", [128, 40], "int32"),
+    "pt": ("sbuf", [128, 20], "int32"),
+    "kf0": ("sbuf", [128, 4], "float32"),
+    "kf1": ("sbuf", [128, 4], "float32"),
+    "of0": ("sbuf", [128, 144], "uint16"),
+    "of1": ("sbuf", [128, 144], "uint16"),
+    "kq0": ("sbuf", [128, 512], CODES), "ks0": ("sbuf", [128, 512], "uint8"),
+    "kq1": ("sbuf", [128, 512], CODES), "ks1": ("sbuf", [128, 512], "uint8"),
+    "xq0": ("sbuf", [128, 256], CODES), "xs0": ("sbuf", [128, 256], "uint8"),
+    "xq1": ("sbuf", [128, 256], CODES), "xs1": ("sbuf", [128, 256], "uint8"),
+    "rq": ("sbuf", [128, 256], CODES), "rs": ("sbuf", [128, 256], "uint8"),
+    "vq0": ("sbuf", [128, 128], CODES), "vs0": ("sbuf", [128, 128], "uint8"),
+    "vq1": ("sbuf", [128, 128], CODES), "vs1": ("sbuf", [128, 128], "uint8"),
+    "vq2": ("sbuf", [128, 128], CODES), "vs2": ("sbuf", [128, 128], "uint8"),
+    "vq3": ("sbuf", [128, 128], CODES), "vs3": ("sbuf", [128, 128], "uint8"),
+    "pw0": ("sbuf", [128, 1024], "float32"),
+    "pw1": ("sbuf", [128, 1024], "float32"),
+    "yo": ("sbuf", [128, 256], "float32"),
+}
+for _p in range(4):
+    SCRATCH["u%d" % _p] = ("sbuf", [128, 1024], "float32")
+    SCRATCH["a%d" % _p] = ("sbuf", [128, 1024], "bfloat16")
+    SCRATCH["aq%d" % _p] = ("sbuf", [128, 256], CODES)
+    SCRATCH["as%d" % _p] = ("sbuf", [128, 256], "uint8")
+for _p in (1, 2):
+    SCRATCH["bq%d" % _p] = ("sbuf", [128, 256], CODES)
+    SCRATCH["bs%d" % _p] = ("sbuf", [128, 256], "uint8")
+for _i in range(8):
+    SCRATCH["ps%d" % _i] = ("psum", [128, 512], "float32")
+
+SEMAPHORES = (["l_ky0", "l_ky1", "l_qx", "l_rt", "l_vv", "l_pos", "q_ky0", "q_ky1", "q_qx", "q_rt", "q_vv", "kf0", "kf1",
+               "n_pp", "n_pt", "n_x", "n_k0", "n_k1", "n_v1", "n_v2", "n_v3", "n_a1", "n_a2", "sent", "ydone", "ycopy", "ystore"]
+              + ["o%d_%d" % (p, b) for p in range(3) for b in range(4)]
+              + ["p%d_%d" % (s, b) for s in range(2) for b in range(4)]
+              + ["c%d_%d" % (s, b) for s in range(2) for b in range(4)]
+              + ["%s%d_%d" % (k, p, b) for k in "sgd" for p in range(4) for b in range(4)]
+              + ["r%d" % p for p in range(4)] + ["q%d" % p for p in range(4)])
+
+
+def rank_program(g, core, T, topo):
+    rank = T.rank_of(core)
+    if rank is None:
+        return
+    mine = topo.cores_of(core)
+    partner = [c for c in T.cores if c != core and c in mine][0]
+    far = [c for c in T.cores if c not in mine]
+    twin = [c for c in far if topo.die(c) == topo.die(core)][0]
+    diag = [c for c in far if c != twin][0]
+    off = topo.engines(core, twin)
+    on = [e for e in topo.engines(core, partner) if e not in off]
+    half = len(off) // 2
+
+    count = {"l_pos": 9 * 16, "n_pp": len(on), "n_pt": len(off), "n_x": 2 * len(on), "n_k0": 2 * len(off), "n_k1": 2 * len(off),
+             "n_v1": 2 * len(on), "n_v2": 2 * half, "n_v3": 2 * half,
+             "n_a1": 2 * len(topo.engines(partner, core)), "n_a2": 2 * len(topo.engines(partner, core)), "ystore": 16}
+    for n in ("ky0", "ky1", "qx", "rt", "vv"):
+        count["l_" + n] = 16
+    seen = set()
+
+    def need(queue, tag, *events):
+        for e in events:
+            if (tag, e) not in seen:
+                seen.add((tag, e))
+                queue.wait_ge(T.sem[e], count.get(e, 1))
+
+    V, S, E = g.vector, g.scalar, g.tensor
+
+    for n, out, src in (("ky0", T.ky_b[:, 0:1024], T.ky[:, 0:1024]), ("qx", T.qx_b[:], T.qx[:]), ("rt", T.rt_b[:], T.rt[:]),
+                        ("ky1", T.ky_b[:, 1024:2048], T.ky[:, 1024:2048]), ("vv", T.vv_b[:], T.vv[:])):
+        S.dma_start(out, src).then_inc(T.sem["l_" + n], 16)
+    g.sync.dma_start(T.pz[:, 0:4], T.kp[:]).then_inc(T.sem["l_pos"], 16)
+    for i in range(8):
+        g.sync.dma_start(T.pz[16 * i:16 * i + 16, 4:20], T.qp[:]).then_inc(T.sem["l_pos"], 16)
+
+    sent = [0]
+
+    def mask(engines):
+        return sum(1 << e for e in engines)
+
+    def xfer(dst, engines, sem, out, src):
+        rid, pid = topo.addr(dst, core)
+        sent[0] += len(engines)
+        return RemoteDMATransfer(dst_ids=[DstId(rid=rid, pnc=pid)], dma_engine_mask=mask(engines), remote_sem=T.sem[sem], srcs=[src], dsts=[out])
+
+    def fused(*transfers):
+        g.remote_dma_fused(list(transfers), local_sem=T.sem.sent)
+
+    def u8(ap):
+        return ap.bitcast(dt.uint8)
+
+    def sends():
+        need(g, "g", "l_pos")
+        fused(xfer(twin, off, "n_pt", T.pt[:, 0:20], T.pz[:, 0:20]), xfer(partner, on, "n_pp", T.pz[:, 20:40], T.pz[:, 0:20]))
+        need(g, "g", "q_ky0", "q_qx")
+        fused(xfer(twin, off, "n_k0", u8(T.kq1[:, 0:256]), u8(T.kq0[:, 0:256])), xfer(partner, on, "n_x", u8(T.xq1[:, 0:256]), u8(T.xq0[:, 0:256])))
+        fused(xfer(twin, off, "n_k0", T.ks1[:, 0:256], T.ks0[:, 0:256]), xfer(partner, on, "n_x", T.xs1[:, 0:256], T.xs0[:, 0:256]))
+        need(g, "g", "q_ky1")
+        fused(xfer(twin, off, "n_k1", u8(T.kq1[:, 256:512]), u8(T.kq0[:, 256:512])))
+        fused(xfer(twin, off, "n_k1", T.ks1[:, 256:512], T.ks0[:, 256:512]))
+        need(g, "g", "q_vv")
+        fused(xfer(twin, off[:half], "n_v2", u8(T.vq2[:, 0:128]), u8(T.vq0[:, 0:128])),
+              xfer(diag, off[half:], "n_v3", u8(T.vq3[:, 0:128]), u8(T.vq0[:, 0:128])),
+              xfer(partner, on, "n_v1", u8(T.vq1[:, 0:128]), u8(T.vq0[:, 0:128])))
+        fused(xfer(twin, off[:half], "n_v2", T.vs2[:, 0:128], T.vs0[:, 0:128]),
+              xfer(diag, off[half:], "n_v3", T.vs3[:, 0:128], T.vs0[:, 0:128]),
+              xfer(partner, on, "n_v1", T.vs1[:, 0:128], T.vs0[:, 0:128]))
+        every = topo.engines(core, partner)
+        for p in (1, 2):
+            need(g, "g", "q%d" % p)
+            fused(xfer(partner, every, "n_a%d" % p, u8(T["bq%d" % p][:, 0:256]), u8(T["aq%d" % p][:, 0:256])))
+            fused(xfer(partner, every, "n_a%d" % p, T["bs%d" % p][:, 0:256], T["as%d" % p][:, 0:256]))
+        g.wait_ge(T.sem.sent, sent[0])
+
+    def quant(name):
+        need(V, "V", "l_" + name)
+        q, s, b, lo, n = {"ky0": ("kq0", "ks0", "ky_b", 0, 256), "ky1": ("kq0", "ks0", "ky_b", 256, 256), "qx": ("xq0", "xs0", "qx_b", 0, 256),
+                          "rt": ("rq", "rs", "rt_b", 0, 256), "vv": ("vq0", "vs0", "vv_b", 0, 128)}[name]
+        V.quantize_mx(T[q][:, lo:lo + n], T[s][:, lo:lo + n], T[b][:, 4 * lo:4 * lo + 4 * n]).then_inc(T.sem["q_" + name], 1)
+
+    def keypos(s):
+        need(V, "V", "n_pt" if s else "l_pos")
+        src = T.pt if s else T.pz
+        V.tensor_scalar(T["kf%d" % s][:], src[:, 0:4], 128.0, None, AluOpType.subtract).then_inc(T.sem["kf%d" % s], 1)
+
+    def offsets(p, b):
+        s = p // 2
+        need(V, "V", "l_pos", "kf%d" % s)
+        if p:
+            need(V, "V", "n_pp")
+        lo, n = ((0, 16), (20, 16), (0, 36))[p]
+        V.tensor_scalar(T["of%d" % s][:, 36 * b + lo:36 * b + lo + n], T.pz[:, 4 + lo:4 + lo + n], T["kf%d" % s][:, b:b + 1], 255.0,
+                        AluOpType.subtract, AluOpType.min).then_inc(T.sem["o%d_%d" % (p, b)], 1)
+
+    keys = (lambda b: ["q_ky%d" % (b // 2)], lambda b: ["n_k%d" % (b // 2)])
+    held = {}
+    turn = {"p": 0, "s": 0}
+    bank = {}
+
+    def take(kind, banks, name, free):
+        k = banks[turn[kind] % len(banks)]
+        turn[kind] += 1
+        if k in held:
+            need(E, "E", held[k])
+        held[k] = free
+        bank[name] = T["ps%d" % k]
+
+    def prod_p(s, b):
+        n = "p%d_%d" % (s, b)
+        take("p", (0, 1, 2), n, "c%d_%d" % (s, b))
+        need(E, "E", "q_rt", *keys[s](b))
+        E.matmul_mx(bank[n][:, 0:256], T["kq%d" % s][:, 128 * b:128 * b + 128], T["ks%d" % s][:, 128 * b:128 * b + 128],
+                    T.rq[:, 0:256], T.rs[:, 0:256], True, True).then_inc(T.sem[n], 1)
+
+    def prod_s(p, b):
+        n, s, x = "s%d_%d" % (p, b), p // 2, int(p in (1, 2))
+        take("s", (3, 4, 5, 6), n, "d%d_%d" % (p, b))
+        need(E, "E", "n_x" if x else "q_qx", *keys[s](b))
+        E.matmul_mx(bank[n][:, 0:256], T["kq%d" % s][:, 128 * b:128 * b + 128], T["ks%d" % s][:, 128 * b:128 * b + 128],
+                    T["xq%d" % x][:, 0:256], T["xs%d" % x][:, 0:256], True, True).then_inc(T.sem[n], 1)
+
+    def copy_p(q, s, b):
+        n = "p%d_%d" % (s, b)
+        out = T["pw%d" % s][:, 256 * b:256 * b + 256]
+        if q == "V":
+            need(V, "V", n)
+            i = V.tensor_copy(out, bank[n][:, 0:256])
+        else:
+            need(S, "S", n)
+            i = S.activation(out, bank[n][:, 0:256], ActivationFunctionType.Copy)
+        i.then_inc(T.sem["c%d_%d" % (s, b)], 1)
+
+    def pick(q, p, b):
+        s = p // 2
+        lo = 36 * b + (20 if p in (1, 2) else 0)
+        out = T["u%d" % p][:, 256 * b:256 * b + 256]
+        src = T["pw%d" % s][:, 256 * b:256 * b + 256].indirect(T["of%d" % s][:, lo:lo + 16])
+        need(V if q == "V" else S, q, "c%d_%d" % (s, b), "o%d_%d" % (min(p, 2), b))
+        i = V.tensor_copy(out, src) if q == "V" else S.activation(out, src, ActivationFunctionType.Copy)
+        i.then_inc(T.sem["g%d_%d" % (p, b)], 1)
+
+    def add(p, b):
+        need(V, "V", "s%d_%d" % (p, b), "g%d_%d" % (p, b))
+        V.tensor_tensor(T["a%d" % p][:, b:1024:4], bank["s%d_%d" % (p, b)][:, 0:256], T["u%d" % p][:, 256 * b:256 * b + 256],
+                        AluOpType.add).then_inc(T.sem["d%d_%d" % (p, b)], 1)
+
+    def finish(p):
+        need(V, "V", *["d%d_%d" % (p, b) for b in range(4)])
+        t = T["a%d" % p]
+        V.tensor_scalar(t[:, 0:1024], t[:, 0:1024], 0.0, 0.03125, AluOpType.max, AluOpType.mult).then_inc(T.sem["r%d" % p], 1)
+        need(V, "V", "r%d" % p)
+        V.quantize_mx(T["aq%d" % p][:, 0:256], T["as%d" % p][:, 0:256], t[:, 0:1024]).then_inc(T.sem["q%d" % p], 1)
+
+    def prod_y(v, a, start, stop, *events):
+        need(E, "E", *events)
+        i = E.matmul_mx(T.ps7[:, 0:256], T["vq%d" % v][:, 0:128], T["vs%d" % v][:, 0:128], T[a % "q"][:, 0:256], T[a % "s"][:, 0:256], start, stop)
+        if stop:
+            i.then_inc(T.sem.ydone, 1)
+
+    for f, i, b in ((prod_p, 0, 0), (prod_p, 0, 1), (prod_s, 0, 0), (prod_p, 0, 2), (prod_p, 0, 3), (prod_s, 0, 1), (prod_s, 0, 2), (prod_s, 0, 3),
+                    (prod_s, 1, 0), (prod_p, 1, 0), (prod_s, 1, 1), (prod_p, 1, 1), (prod_s, 1, 2), (prod_s, 1, 3), (prod_p, 1, 2), (prod_p, 1, 3),
+                    (prod_s, 2, 0), (prod_s, 2, 1), (prod_s, 2, 2), (prod_s, 2, 3), (prod_s, 3, 0), (prod_s, 3, 1), (prod_s, 3, 2), (prod_s, 3, 3)):
+        f(i, b)
+    prod_y(0, "a%s0", True, False, "q_vv", "q0")
+    prod_y(1, "b%s1", False, False, "n_v1", "n_a1")
+    prod_y(2, "a%s3", False, False, "n_v2", "q3")
+    prod_y(3, "b%s2", False, True, "n_v3", "n_a2")
+
+    quant("ky0")
+    quant("qx")
+    keypos(0)
+    for b in range(4):
+        offsets(0, b)
+    quant("rt")
+    quant("ky1")
+    pick("V", 0, 0)
+    copy_p("V", 0, 3)
+    quant("vv")
+    for b in range(3):
+        add(0, b)
+    for b in range(4):
+        offsets(1, b)
+    add(0, 3)
+    finish(0)
+    keypos(1)
+    for b in range(4):
+        offsets(2, b)
+    for b in range(4):
+        add(1, b)
+    finish(1)
+    pick("V", 2, 0)
+    for p in (2, 3):
+        for b in range(4):
+            add(p, b)
+        finish(p)
+
+    for f, i, b in ((copy_p, 0, 0), (copy_p, 0, 1), (pick, 0, 1), (copy_p, 0, 2), (pick, 0, 2), (pick, 0, 3),
+                    (pick, 1, 0), (pick, 1, 1), (pick, 1, 2), (copy_p, 1, 0), (pick, 1, 3), (copy_p, 1, 1), (pick, 2, 1), (copy_p, 1, 2), (copy_p, 1, 3),
+                    (pick, 2, 2), (pick, 2, 3), (pick, 3, 0), (pick, 3, 1), (pick, 3, 2), (pick, 3, 3)):
+        f("S", i, b)
+    need(S, "S", "ydone")
+    S.activation(T.yo[:], T.ps7[:, 0:256], ActivationFunctionType.Copy).then_inc(T.sem.ycopy, 1)
+
+    sends()
+    g.sync.wait_ge(T.sem.ycopy, 1)
+    g.sync.dma_start(T.y[:], T.yo[:]).then_inc(T.sem.ystore, 16)
+    g.sync.wait_ge(T.sem.ystore, 16)

@@ -7,62 +7,82 @@ SCRATCH = {
     "qx_b": ("sbuf", [128, 1024], "bfloat16"),
     "rt_b": ("sbuf", [128, 1024], "bfloat16"),
     "vv_b": ("sbuf", [128, 512], "bfloat16"),
-    "pz": ("sbuf", [128, 40], "int32"),
-    "pt": ("sbuf", [128, 20], "int32"),
-    "kf0": ("sbuf", [128, 4], "float32"),
-    "kf1": ("sbuf", [128, 4], "float32"),
-    "of0": ("sbuf", [128, 144], "uint16"),
-    "of1": ("sbuf", [128, 144], "uint16"),
+    "pz": ("sbuf", [128, 20], "int32"),
+    "pu": ("sbuf", [128, 20], "uint16"),
+    "pt": ("sbuf", [128, 20], "uint16"),
+    "ph": ("sbuf", [128, 20], "uint16"),
+    "pp": ("sbuf", [128, 20], "uint16"),
+    "kf": ("sbuf", [128, 4], "float32"),
+    "of0": ("sbuf", [128, 64], "uint16"),
+    "of1": ("sbuf", [128, 64], "uint16"),
     "kq0": ("sbuf", [128, 512], CODES), "ks0": ("sbuf", [128, 512], "uint8"),
     "kq1": ("sbuf", [128, 512], CODES), "ks1": ("sbuf", [128, 512], "uint8"),
     "xq0": ("sbuf", [128, 256], CODES), "xs0": ("sbuf", [128, 256], "uint8"),
     "xq1": ("sbuf", [128, 256], CODES), "xs1": ("sbuf", [128, 256], "uint8"),
     "rq": ("sbuf", [128, 256], CODES), "rs": ("sbuf", [128, 256], "uint8"),
-    "vq0": ("sbuf", [128, 128], CODES), "vs0": ("sbuf", [128, 128], "uint8"),
-    "vq1": ("sbuf", [128, 128], CODES), "vs1": ("sbuf", [128, 128], "uint8"),
-    "vq2": ("sbuf", [128, 128], CODES), "vs2": ("sbuf", [128, 128], "uint8"),
-    "vq3": ("sbuf", [128, 128], CODES), "vs3": ("sbuf", [128, 128], "uint8"),
-    "pw0": ("sbuf", [128, 1024], "float32"),
-    "pw1": ("sbuf", [128, 1024], "float32"),
+    "pw": ("sbuf", [128, 1024], "float32"),
     "yo": ("sbuf", [128, 256], "float32"),
 }
-for _p in range(4):
+for _i in range(4):
+    SCRATCH["vq%d" % _i] = ("sbuf", [128, 128], CODES)
+    SCRATCH["vs%d" % _i] = ("sbuf", [128, 128], "uint8")
+for _p in range(2):
     SCRATCH["u%d" % _p] = ("sbuf", [128, 1024], "float32")
     SCRATCH["a%d" % _p] = ("sbuf", [128, 1024], "bfloat16")
     SCRATCH["aq%d" % _p] = ("sbuf", [128, 256], CODES)
     SCRATCH["as%d" % _p] = ("sbuf", [128, 256], "uint8")
-for _p in (1, 2):
-    SCRATCH["bq%d" % _p] = ("sbuf", [128, 256], CODES)
-    SCRATCH["bs%d" % _p] = ("sbuf", [128, 256], "uint8")
+for _p in "pth":
+    SCRATCH["bq_" + _p] = ("sbuf", [128, 256], CODES)
+    SCRATCH["bs_" + _p] = ("sbuf", [128, 256], "uint8")
 for _i in range(8):
     SCRATCH["ps%d" % _i] = ("psum", [128, 512], "float32")
 
-SEMAPHORES = (["l_ky0", "l_ky1", "l_qx", "l_rt", "l_vv", "l_pos", "q_ky0", "q_ky1", "q_qx", "q_rt", "q_vv", "kf0", "kf1",
-               "n_pp", "n_pt", "n_x", "n_k0", "n_k1", "n_v1", "n_v2", "n_v3", "n_a1", "n_a2", "sent", "ydone", "ycopy", "ystore"]
-              + ["o%d_%d" % (p, b) for p in range(3) for b in range(4)]
-              + ["p%d_%d" % (s, b) for s in range(2) for b in range(4)]
-              + ["c%d_%d" % (s, b) for s in range(2) for b in range(4)]
-              + ["%s%d_%d" % (k, p, b) for k in "sgd" for p in range(4) for b in range(4)]
-              + ["r%d" % p for p in range(4)] + ["q%d" % p for p in range(4)])
+SEMAPHORES = (["l_ky0", "l_ky1", "l_qx", "l_rt", "l_vv", "l_pos", "q_ky0", "q_ky1", "q_qx", "q_rt", "q_vv", "pu", "kf",
+               "n_pt", "n_ph", "n_pp", "n_k0", "n_k1", "n_r", "n_x", "n_v1", "n_v2", "n_v3", "n_ap", "n_at", "n_ah", "sent",
+               "ydone", "ycopy", "ystore", "q0", "q1"]
+              + ["p%d" % b for b in range(4)] + ["c%d" % b for b in range(4)]
+              + ["%s%d_%d" % (k, p, b) for k in "osgdr" for p in range(2) for b in range(4)])
+
+LOADS = ["ky0", "rt", "ky1", "qx", "vv"]
+QUANTS = ["ky0", "rt", "ky1", "qx"]
+SENDS = ["k0", "r", "k1", "x", "v"]
+TENSOR = ["p0 p1 s00 s01 p2 p3 s02 s03 s10 s11 s12 s13", "p0 p1 s%0 s%1 p2 p3 s%2 s%3"]
+SCALAR = ["c0 g00 g01 c2 g02 g03 g10 g11 g12 g13 r10 r11 r12", "c0 g%0 c2 g%2 r%0 r%1 r%2"]
+VECTOR = ["kf o00 o01 o02 o03 c1 d00 r00 d01 r01 c3 qvv o10 o11 o12 o13 d02 r02 d03 r03 q0 d10 d11 d12 d13 r13 q1",
+          "kf o%0 o%1 o%2 o%3 c1 g%1 d%0 d%1 c3 g%3 d%2 d%3 r%3 q%"]
+YORDER = ["own", "p", "t", "h"]
 
 
 def rank_program(g, core, T, topo):
-    rank = T.rank_of(core)
-    if rank is None:
+    here = topo.cores_of(core)
+    ranks = [c for c in T.cores if c in here]
+    if not ranks:
         return
-    mine = topo.cores_of(core)
-    partner = [c for c in T.cores if c != core and c in mine][0]
-    far = [c for c in T.cores if c not in mine]
-    twin = [c for c in far if topo.die(c) == topo.die(core)][0]
+
+    def team(r):
+        return [r] + [c for c in topo.cores_of(r) if topo.die(c) == topo.die(r) and c != r][:2]
+
+    own = [c for c in ranks if topo.die(c) == topo.die(core)][0]
+    if core not in team(own):
+        return
+    role = team(own).index(core)
+    is_rank = role == 0
+    partner = [c for c in ranks if c != own][0]
+    far = [c for c in T.cores if c not in here]
+    twin = [c for c in far if topo.die(c) == topo.die(own)][0]
     diag = [c for c in far if c != twin][0]
-    off = topo.engines(core, twin)
-    on = [e for e in topo.engines(core, partner) if e not in off]
+    off = topo.engines(own, twin)
+    every = topo.engines(own, partner)
+    on = [e for e in every if e not in off]
     half = len(off) // 2
 
-    count = {"l_pos": 9 * 16, "n_pp": len(on), "n_pt": len(off), "n_x": 2 * len(on), "n_k0": 2 * len(off), "n_k1": 2 * len(off),
-             "n_v1": 2 * len(on), "n_v2": 2 * half, "n_v3": 2 * half,
-             "n_a1": 2 * len(topo.engines(partner, core)), "n_a2": 2 * len(topo.engines(partner, core)), "ystore": 16}
-    for n in ("ky0", "ky1", "qx", "rt", "vv"):
+    direct = role == 1
+    count = {"l_pos": 9 * 16, "ystore": 16, "n_pt": len(off if direct else every), "n_ph": half, "n_pp": len(every) if is_rank else half,
+             "n_k0": 2 * len(off if direct else every), "n_k1": 2 * len(off if direct else every), "n_r": 2 * len(on if direct else every),
+             "n_x": 2 * (len(off) if is_rank else half), "n_v1": 2 * len(on), "n_v2": 2 * half, "n_v3": 2 * half}
+    for n in ("n_ap", "n_at", "n_ah"):
+        count[n] = 2 * len(every)
+    for n in LOADS:
         count["l_" + n] = 16
     seen = set()
 
@@ -73,52 +93,59 @@ def rank_program(g, core, T, topo):
                 queue.wait_ge(T.sem[e], count.get(e, 1))
 
     V, S, E = g.vector, g.scalar, g.tensor
-
-    for n, out, src in (("ky0", T.ky_b[:, 0:1024], T.ky[:, 0:1024]), ("qx", T.qx_b[:], T.qx[:]), ("rt", T.rt_b[:], T.rt[:]),
-                        ("ky1", T.ky_b[:, 1024:2048], T.ky[:, 1024:2048]), ("vv", T.vv_b[:], T.vv[:])):
-        S.dma_start(out, src).then_inc(T.sem["l_" + n], 16)
-    g.sync.dma_start(T.pz[:, 0:4], T.kp[:]).then_inc(T.sem["l_pos"], 16)
-    for i in range(8):
-        g.sync.dma_start(T.pz[16 * i:16 * i + 16, 4:20], T.qp[:]).then_inc(T.sem["l_pos"], 16)
-
     sent = [0]
-
-    def mask(engines):
-        return sum(1 << e for e in engines)
 
     def xfer(dst, engines, sem, out, src):
         rid, pid = topo.addr(dst, core)
         sent[0] += len(engines)
-        return RemoteDMATransfer(dst_ids=[DstId(rid=rid, pnc=pid)], dma_engine_mask=mask(engines), remote_sem=T.sem[sem], srcs=[src], dsts=[out])
+        return RemoteDMATransfer(dst_ids=[DstId(rid=rid, pnc=pid)], dma_engine_mask=sum(1 << e for e in engines), remote_sem=T.sem[sem], srcs=[src], dsts=[out])
 
     def fused(*transfers):
         g.remote_dma_fused(list(transfers), local_sem=T.sem.sent)
 
-    def u8(ap):
-        return ap.bitcast(dt.uint8)
+    def view(n, name, lo, hi):
+        return T[name % n][:, lo:hi].bitcast(dt.uint8) if n == "q" else T[name % n][:, lo:hi]
 
-    def sends():
-        need(g, "g", "l_pos")
-        fused(xfer(twin, off, "n_pt", T.pt[:, 0:20], T.pz[:, 0:20]), xfer(partner, on, "n_pp", T.pz[:, 20:40], T.pz[:, 0:20]))
-        need(g, "g", "q_ky0", "q_qx")
-        fused(xfer(twin, off, "n_k0", u8(T.kq1[:, 0:256]), u8(T.kq0[:, 0:256])), xfer(partner, on, "n_x", u8(T.xq1[:, 0:256]), u8(T.xq0[:, 0:256])))
-        fused(xfer(twin, off, "n_k0", T.ks1[:, 0:256], T.ks0[:, 0:256]), xfer(partner, on, "n_x", T.xs1[:, 0:256], T.xs0[:, 0:256]))
-        need(g, "g", "q_ky1")
-        fused(xfer(twin, off, "n_k1", u8(T.kq1[:, 256:512]), u8(T.kq0[:, 256:512])))
-        fused(xfer(twin, off, "n_k1", T.ks1[:, 256:512], T.ks0[:, 256:512]))
-        need(g, "g", "q_vv")
-        fused(xfer(twin, off[:half], "n_v2", u8(T.vq2[:, 0:128]), u8(T.vq0[:, 0:128])),
-              xfer(diag, off[half:], "n_v3", u8(T.vq3[:, 0:128]), u8(T.vq0[:, 0:128])),
-              xfer(partner, on, "n_v1", u8(T.vq1[:, 0:128]), u8(T.vq0[:, 0:128])))
-        fused(xfer(twin, off[:half], "n_v2", T.vs2[:, 0:128], T.vs0[:, 0:128]),
-              xfer(diag, off[half:], "n_v3", T.vs3[:, 0:128], T.vs0[:, 0:128]),
-              xfer(partner, on, "n_v1", T.vs1[:, 0:128], T.vs0[:, 0:128]))
-        every = topo.engines(core, partner)
-        for p in (1, 2):
-            need(g, "g", "q%d" % p)
-            fused(xfer(partner, every, "n_a%d" % p, u8(T["bq%d" % p][:, 0:256]), u8(T["aq%d" % p][:, 0:256])))
-            fused(xfer(partner, every, "n_a%d" % p, T["bs%d" % p][:, 0:256], T["as%d" % p][:, 0:256]))
-        g.wait_ge(T.sem.sent, sent[0])
+    def put(n, dst, engines, sem, out, src, lo=0, hi=256):
+        return xfer(dst, engines, sem, view(n, out, lo, hi), view(n, src, lo, hi))
+
+    def positions(dst, engines, sem, out, src):
+        return xfer(dst, engines, sem, T[out][:, 0:20], T[src][:, 0:20])
+
+    def tile_out(p, dst, key):
+        need(g, "g", "q%d" % p)
+        for n in "qs":
+            fused(put(n, dst, every, "n_a" + key, "b%s_" + key, "a%s" + str(p)))
+
+    def send(what):
+        if what in ("k0", "k1"):
+            need(g, "g", "q_ky" + what[1])
+            lo = 256 * int(what[1])
+            for n in "qs":
+                fused(put(n, team(twin)[1], off, "n_" + what, "k%s1", "k%s0", lo, lo + 256))
+        if what == "r":
+            need(g, "g", "q_rt")
+            for n in "qs":
+                fused(put(n, team(own)[1], on, "n_r", "r%s", "r%s"))
+        if what == "x":
+            need(g, "g", "q_qx")
+            for n in "qs":
+                fused(put(n, team(own)[1], on[:half], "n_x", "x%s0", "x%s0"), put(n, team(partner)[2], on[half:], "n_x", "x%s1", "x%s0"),
+                      put(n, partner, off, "n_x", "x%s1", "x%s0"))
+        if what == "v":
+            need(g, "g", "q_vv")
+            for n in "qs":
+                fused(put(n, twin, off[:half], "n_v2", "v%s2", "v%s0", 0, 128), put(n, diag, off[half:], "n_v3", "v%s3", "v%s0", 0, 128),
+                      put(n, partner, on, "n_v1", "v%s1", "v%s0", 0, 128))
+
+    if is_rank:
+        g.sync.dma_start(T.pz[:, 0:4], T.kp[:]).then_inc(T.sem["l_pos"], 16)
+        for i in range(8):
+            (S if i % 2 else g.sync).dma_start(T.pz[16 * i:16 * i + 16, 4:20], T.qp[:]).then_inc(T.sem["l_pos"], 16)
+        for n in LOADS:
+            out, src = {"ky0": (T.ky_b[:, 0:1024], T.ky[:, 0:1024]), "ky1": (T.ky_b[:, 1024:2048], T.ky[:, 1024:2048]), "rt": (T.rt_b[:], T.rt[:]),
+                        "qx": (T.qx_b[:], T.qx[:]), "vv": (T.vv_b[:], T.vv[:])}[n]
+            S.dma_start(out, src).then_inc(T.sem["l_" + n], 16)
 
     def quant(name):
         need(V, "V", "l_" + name)
@@ -126,64 +153,43 @@ def rank_program(g, core, T, topo):
                           "rt": ("rq", "rs", "rt_b", 0, 256), "vv": ("vq0", "vs0", "vv_b", 0, 128)}[name]
         V.quantize_mx(T[q][:, lo:lo + n], T[s][:, lo:lo + n], T[b][:, 4 * lo:4 * lo + 4 * n]).then_inc(T.sem["q_" + name], 1)
 
-    def keypos(s):
-        need(V, "V", "n_pt" if s else "l_pos")
-        src = T.pt if s else T.pz
-        V.tensor_scalar(T["kf%d" % s][:], src[:, 0:4], 128.0, None, AluOpType.subtract).then_inc(T.sem["kf%d" % s], 1)
+    KQ, KS = (T.kq0, T.ks0) if is_rank else (T.kq1, T.ks1)
+    key_pos = (T.pu, "pu") if is_rank else (T.pt, "n_pt")
+    query_pos = ((T.pu, "pu") if is_rank else (T.ph, "n_ph"), (T.pp, "n_pp"))
+    query_ready = ("q_qx" if is_rank else "n_x", "n_x")
+    rt_ready = "q_rt" if is_rank else "n_r"
+    held, turn, bank = {}, {"p": 0, "s": 0}, {}
+
+    def keypos():
+        need(V, "V", key_pos[1])
+        V.tensor_scalar(T.kf[:], key_pos[0][:, 0:4], 128.0, None, AluOpType.subtract).then_inc(T.sem.kf, 1)
 
     def offsets(p, b):
-        s = p // 2
-        need(V, "V", "l_pos", "kf%d" % s)
-        if p:
-            need(V, "V", "n_pp")
-        lo, n = ((0, 16), (20, 16), (0, 36))[p]
-        V.tensor_scalar(T["of%d" % s][:, 36 * b + lo:36 * b + lo + n], T.pz[:, 4 + lo:4 + lo + n], T["kf%d" % s][:, b:b + 1], 255.0,
+        need(V, "V", query_pos[p][1], "kf")
+        V.tensor_scalar(T["of%d" % p][:, 16 * b:16 * b + 16], query_pos[p][0][:, 4:20], T.kf[:, b:b + 1], 255.0,
                         AluOpType.subtract, AluOpType.min).then_inc(T.sem["o%d_%d" % (p, b)], 1)
 
-    keys = (lambda b: ["q_ky%d" % (b // 2)], lambda b: ["n_k%d" % (b // 2)])
-    held = {}
-    turn = {"p": 0, "s": 0}
-    bank = {}
-
-    def take(kind, banks, name, free):
+    def product(kind, banks, name, free, b, moving, ready):
         k = banks[turn[kind] % len(banks)]
         turn[kind] += 1
         if k in held:
             need(E, "E", held[k])
         held[k] = free
         bank[name] = T["ps%d" % k]
+        need(E, "E", ready, ("q_ky%d" if is_rank else "n_k%d") % (b // 2))
+        E.matmul_mx(bank[name][:, 0:256], KQ[:, 128 * b:128 * b + 128], KS[:, 128 * b:128 * b + 128],
+                    T[moving % "q"][:, 0:256], T[moving % "s"][:, 0:256], True, True).then_inc(T.sem[name], 1)
 
-    def prod_p(s, b):
-        n = "p%d_%d" % (s, b)
-        take("p", (0, 1, 2), n, "c%d_%d" % (s, b))
-        need(E, "E", "q_rt", *keys[s](b))
-        E.matmul_mx(bank[n][:, 0:256], T["kq%d" % s][:, 128 * b:128 * b + 128], T["ks%d" % s][:, 128 * b:128 * b + 128],
-                    T.rq[:, 0:256], T.rs[:, 0:256], True, True).then_inc(T.sem[n], 1)
-
-    def prod_s(p, b):
-        n, s, x = "s%d_%d" % (p, b), p // 2, int(p in (1, 2))
-        take("s", (3, 4, 5, 6), n, "d%d_%d" % (p, b))
-        need(E, "E", "n_x" if x else "q_qx", *keys[s](b))
-        E.matmul_mx(bank[n][:, 0:256], T["kq%d" % s][:, 128 * b:128 * b + 128], T["ks%d" % s][:, 128 * b:128 * b + 128],
-                    T["xq%d" % x][:, 0:256], T["xs%d" % x][:, 0:256], True, True).then_inc(T.sem[n], 1)
-
-    def copy_p(q, s, b):
-        n = "p%d_%d" % (s, b)
-        out = T["pw%d" % s][:, 256 * b:256 * b + 256]
-        if q == "V":
-            need(V, "V", n)
-            i = V.tensor_copy(out, bank[n][:, 0:256])
-        else:
-            need(S, "S", n)
-            i = S.activation(out, bank[n][:, 0:256], ActivationFunctionType.Copy)
-        i.then_inc(T.sem["c%d_%d" % (s, b)], 1)
+    def copy_p(q, b):
+        need(V if q == "V" else S, q, "p%d" % b)
+        out, src = T.pw[:, 256 * b:256 * b + 256], bank["p%d" % b][:, 0:256]
+        i = V.tensor_copy(out, src) if q == "V" else S.activation(out, src, ActivationFunctionType.Copy)
+        i.then_inc(T.sem["c%d" % b], 1)
 
     def pick(q, p, b):
-        s = p // 2
-        lo = 36 * b + (20 if p in (1, 2) else 0)
         out = T["u%d" % p][:, 256 * b:256 * b + 256]
-        src = T["pw%d" % s][:, 256 * b:256 * b + 256].indirect(T["of%d" % s][:, lo:lo + 16])
-        need(V if q == "V" else S, q, "c%d_%d" % (s, b), "o%d_%d" % (min(p, 2), b))
+        src = T.pw[:, 256 * b:256 * b + 256].indirect(T["of%d" % p][:, 16 * b:16 * b + 16])
+        need(V if q == "V" else S, q, "c%d" % b, "o%d_%d" % (p, b))
         i = V.tensor_copy(out, src) if q == "V" else S.activation(out, src, ActivationFunctionType.Copy)
         i.then_inc(T.sem["g%d_%d" % (p, b)], 1)
 
@@ -192,64 +198,84 @@ def rank_program(g, core, T, topo):
         V.tensor_tensor(T["a%d" % p][:, b:1024:4], bank["s%d_%d" % (p, b)][:, 0:256], T["u%d" % p][:, 256 * b:256 * b + 256],
                         AluOpType.add).then_inc(T.sem["d%d_%d" % (p, b)], 1)
 
-    def finish(p):
-        need(V, "V", *["d%d_%d" % (p, b) for b in range(4)])
-        t = T["a%d" % p]
-        V.tensor_scalar(t[:, 0:1024], t[:, 0:1024], 0.0, 0.03125, AluOpType.max, AluOpType.mult).then_inc(T.sem["r%d" % p], 1)
-        need(V, "V", "r%d" % p)
-        V.quantize_mx(T["aq%d" % p][:, 0:256], T["as%d" % p][:, 0:256], t[:, 0:1024]).then_inc(T.sem["q%d" % p], 1)
+    def relu(q, p, b):
+        need(V if q == "V" else S, q, "d%d_%d" % (p, b))
+        t = T["a%d" % p][:, b:1024:4]
+        if q == "V":
+            i = V.tensor_scalar(t, t, 0.0, 0.03125, AluOpType.max, AluOpType.mult)
+        else:
+            i = S.activation(t, t, ActivationFunctionType.Relu, scale=0.03125)
+        i.then_inc(T.sem["r%d_%d" % (p, b)], 1)
 
-    def prod_y(v, a, start, stop, *events):
-        need(E, "E", *events)
-        i = E.matmul_mx(T.ps7[:, 0:256], T["vq%d" % v][:, 0:128], T["vs%d" % v][:, 0:128], T[a % "q"][:, 0:256], T[a % "s"][:, 0:256], start, stop)
-        if stop:
-            i.then_inc(T.sem.ydone, 1)
+    def quant_a(p):
+        need(V, "V", *["r%d_%d" % (p, b) for b in range(4)])
+        V.quantize_mx(T["aq%d" % p][:, 0:256], T["as%d" % p][:, 0:256], T["a%d" % p][:, 0:1024]).then_inc(T.sem["q%d" % p], 1)
 
-    for f, i, b in ((prod_p, 0, 0), (prod_p, 0, 1), (prod_s, 0, 0), (prod_p, 0, 2), (prod_p, 0, 3), (prod_s, 0, 1), (prod_s, 0, 2), (prod_s, 0, 3),
-                    (prod_s, 1, 0), (prod_p, 1, 0), (prod_s, 1, 1), (prod_p, 1, 1), (prod_s, 1, 2), (prod_s, 1, 3), (prod_p, 1, 2), (prod_p, 1, 3),
-                    (prod_s, 2, 0), (prod_s, 2, 1), (prod_s, 2, 2), (prod_s, 2, 3), (prod_s, 3, 0), (prod_s, 3, 1), (prod_s, 3, 2), (prod_s, 3, 3)):
-        f(i, b)
-    prod_y(0, "a%s0", True, False, "q_vv", "q0")
-    prod_y(1, "b%s1", False, False, "n_v1", "n_a1")
-    prod_y(2, "a%s3", False, False, "n_v2", "q3")
-    prod_y(3, "b%s2", False, True, "n_v3", "n_a2")
+    def steps(q, text):
+        for w in text.replace("%", str(role - 1)).split():
+            k, d = w[0], [int(c) for c in w[1:] if c.isdigit()]
+            if w == "kf":
+                keypos()
+            elif w == "qvv":
+                quant("vv")
+            elif k == "q":
+                quant_a(d[0])
+            elif k == "p":
+                product("p", (0, 1, 2), "p%d" % d[0], "c%d" % d[0], d[0], "r%s", rt_ready)
+            elif k == "s":
+                product("s", (3, 4, 5, 6), "s%d_%d" % (d[0], d[1]), "d%d_%d" % (d[0], d[1]), d[1], "x%s" + str(d[0]), query_ready[d[0]])
+            elif k == "c":
+                copy_p(q, d[0])
+            elif k == "g":
+                pick(q, d[0], d[1])
+            elif k == "o":
+                offsets(d[0], d[1])
+            elif k == "d":
+                add(d[0], d[1])
+            elif k == "r":
+                relu(q, d[0], d[1])
 
-    quant("ky0")
-    quant("qx")
-    keypos(0)
-    for b in range(4):
-        offsets(0, b)
-    quant("rt")
-    quant("ky1")
-    pick("V", 0, 0)
-    copy_p("V", 0, 3)
-    quant("vv")
-    for b in range(3):
-        add(0, b)
-    for b in range(4):
-        offsets(1, b)
-    add(0, 3)
-    finish(0)
-    keypos(1)
-    for b in range(4):
-        offsets(2, b)
-    for b in range(4):
-        add(1, b)
-    finish(1)
-    pick("V", 2, 0)
-    for p in (2, 3):
-        for b in range(4):
-            add(p, b)
-        finish(p)
+    if is_rank:
+        need(V, "V", "l_pos")
+        V.tensor_copy(T.pu[:], T.pz[:]).then_inc(T.sem.pu, 1)
+        for n in QUANTS:
+            quant(n)
+    kind = min(role, 1)
+    steps("E", TENSOR[kind])
+    steps("V", VECTOR[kind])
+    steps("S", SCALAR[kind])
 
-    for f, i, b in ((copy_p, 0, 0), (copy_p, 0, 1), (pick, 0, 1), (copy_p, 0, 2), (pick, 0, 2), (pick, 0, 3),
-                    (pick, 1, 0), (pick, 1, 1), (pick, 1, 2), (copy_p, 1, 0), (pick, 1, 3), (copy_p, 1, 1), (pick, 2, 1), (copy_p, 1, 2), (copy_p, 1, 3),
-                    (pick, 2, 2), (pick, 2, 3), (pick, 3, 0), (pick, 3, 1), (pick, 3, 2), (pick, 3, 3)):
-        f("S", i, b)
-    need(S, "S", "ydone")
-    S.activation(T.yo[:], T.ps7[:, 0:256], ActivationFunctionType.Copy).then_inc(T.sem.ycopy, 1)
-
-    sends()
-    g.sync.wait_ge(T.sem.ycopy, 1)
-    g.sync.dma_start(T.y[:], T.yo[:]).then_inc(T.sem.ystore, 16)
-    g.sync.wait_ge(T.sem.ystore, 16)
+    if role == 1:
+        need(g, "g", "n_pt")
+        fused(positions(team(own)[2], every, "n_pt", "pt", "pt"))
+        need(g, "g", "n_r")
+        for n in "qs":
+            fused(put(n, team(own)[2], every, "n_r", "r%s", "r%s"))
+        for h in range(2):
+            need(g, "g", "n_k%d" % h)
+            for n in "qs":
+                fused(put(n, team(own)[2], every, "n_k%d" % h, "k%s1", "k%s1", 256 * h, 256 * h + 256))
+        tile_out(0, own, "t")
+    elif role == 2:
+        need(g, "g", "n_pp")
+        fused(positions(own, every, "n_pp", "pp", "pp"))
+        tile_out(1, partner, "h")
+    else:
+        need(g, "g", "pu")
+        fused(positions(team(twin)[1], off, "n_pt", "pt", "pu"), positions(team(own)[1], on[:half], "n_ph", "ph", "pu"),
+              positions(team(partner)[2], on[half:], "n_pp", "pp", "pu"))
+        for what in SENDS:
+            send(what)
+        tile_out(1, partner, "p")
+        source = {"own": (0, "a%s0", "q_vv", "q0"), "p": (1, "b%s_p", "n_v1", "n_ap"), "t": (2, "b%s_t", "n_v2", "n_at"), "h": (3, "b%s_h", "n_v3", "n_ah")}
+        for i, name in enumerate(YORDER):
+            v, a, ready, made = source[name]
+            need(E, "E", ready, made)
+            y = E.matmul_mx(T.ps7[:, 0:256], T["vq%d" % v][:, 0:128], T["vs%d" % v][:, 0:128], T[a % "q"][:, 0:256], T[a % "s"][:, 0:256], i == 0, i == 3)
+        y.then_inc(T.sem.ydone, 1)
+        need(S, "S", "ydone")
+        S.activation(T.yo[:], T.ps7[:, 0:256], ActivationFunctionType.Copy).then_inc(T.sem.ycopy, 1)
+        g.sync.wait_ge(T.sem.ycopy, 1)
+        g.sync.dma_start(T.y[:], T.yo[:]).then_inc(T.sem.ystore, 16)
+        g.sync.wait_ge(T.sem.ystore, 16)
+    g.wait_ge(T.sem.sent, sent[0])

from concourse.bass import DstId, RemoteDMATransfer
from concourse.mybir import dt, AluOpType, ActivationFunctionType

CODES = "float8_e4m3fn_x4"
SCRATCH = {
    "ky_b": ("sbuf", [128, 2048], "bfloat16"),
    "qx_b": ("sbuf", [128, 1024], "bfloat16"),
    "rt_b": ("sbuf", [128, 1024], "bfloat16"),
    "vv_b": ("sbuf", [128, 512], "bfloat16"),
    "pz": ("sbuf", [128, 20], "int32"),
    "pu": ("sbuf", [128, 20], "uint16"),
    "pt": ("sbuf", [128, 20], "uint16"),
    "ph": ("sbuf", [128, 20], "uint16"),
    "pp": ("sbuf", [128, 20], "uint16"),
    "kf": ("sbuf", [128, 4], "float32"),
    "of0": ("sbuf", [128, 64], "uint16"),
    "of1": ("sbuf", [128, 64], "uint16"),
    "kq0": ("sbuf", [128, 512], CODES), "ks0": ("sbuf", [128, 512], "uint8"),
    "kq1": ("sbuf", [128, 512], CODES), "ks1": ("sbuf", [128, 512], "uint8"),
    "xq0": ("sbuf", [128, 256], CODES), "xs0": ("sbuf", [128, 256], "uint8"),
    "xq1": ("sbuf", [128, 256], CODES), "xs1": ("sbuf", [128, 256], "uint8"),
    "rq": ("sbuf", [128, 256], CODES), "rs": ("sbuf", [128, 256], "uint8"),
    "pw": ("sbuf", [128, 1024], "float32"),
    "yo": ("sbuf", [128, 256], "float32"),
}
for _i in range(4):
    SCRATCH["vq%d" % _i] = ("sbuf", [128, 128], CODES)
    SCRATCH["vs%d" % _i] = ("sbuf", [128, 128], "uint8")
for _p in range(2):
    SCRATCH["u%d" % _p] = ("sbuf", [128, 1024], "float32")
    SCRATCH["a%d" % _p] = ("sbuf", [128, 1024], "bfloat16")
    SCRATCH["aq%d" % _p] = ("sbuf", [128, 256], CODES)
    SCRATCH["as%d" % _p] = ("sbuf", [128, 256], "uint8")
for _p in "pth":
    SCRATCH["bq_" + _p] = ("sbuf", [128, 256], CODES)
    SCRATCH["bs_" + _p] = ("sbuf", [128, 256], "uint8")
for _i in range(8):
    SCRATCH["ps%d" % _i] = ("psum", [128, 512], "float32")

SEMAPHORES = (["l_ky0", "l_ky1", "l_qx", "l_rt", "l_vv", "l_pos", "q_ky0", "q_ky1", "q_qx", "q_rt", "q_vv", "pu", "kf",
               "n_pt", "n_ph", "n_pp", "n_k0", "n_k1", "n_r", "n_x", "n_v1", "n_v2", "n_v3", "n_ap", "n_at", "n_ah", "sent",
               "ydone", "ycopy", "ystore", "q0", "q1"]
              + ["p%d" % b for b in range(4)] + ["c%d" % b for b in range(4)]
              + ["%s%d_%d" % (k, p, b) for k in "osgdr" for p in range(2) for b in range(4)])

LOADS = ["ky0", "rt", "ky1", "qx", "vv"]
QUANTS = ["ky0", "rt", "ky1", "qx"]
SENDS = ["k0", "r", "k1", "x", "v"]
TENSOR = ["p0 p1 s00 s01 p2 p3 s02 s03 s10 s11 s12 s13", "p0 p1 s%0 s%1 p2 p3 s%2 s%3"]
SCALAR = ["c0 g00 g01 c2 g02 g03 g10 g11 g12 g13 r10 r11 r12", "c0 g%0 c2 g%2 r%0 r%1 r%2"]
VECTOR = ["kf o00 o01 o02 o03 c1 d00 r00 d01 r01 c3 qvv o10 o11 o12 o13 d02 r02 d03 r03 q0 d10 d11 d12 d13 r13 q1",
          "kf o%0 o%1 o%2 o%3 c1 g%1 d%0 d%1 c3 g%3 d%2 d%3 r%3 q%"]
YORDER = ["own", "p", "t", "h"]


def rank_program(g, core, T, topo):
    here = topo.cores_of(core)
    ranks = [c for c in T.cores if c in here]
    if not ranks:
        return

    def team(r):
        return [r] + [c for c in topo.cores_of(r) if topo.die(c) == topo.die(r) and c != r][:2]

    own = [c for c in ranks if topo.die(c) == topo.die(core)][0]
    if core not in team(own):
        return
    role = team(own).index(core)
    is_rank = role == 0
    partner = [c for c in ranks if c != own][0]
    far = [c for c in T.cores if c not in here]
    twin = [c for c in far if topo.die(c) == topo.die(own)][0]
    diag = [c for c in far if c != twin][0]
    off = topo.engines(own, twin)
    every = topo.engines(own, partner)
    on = [e for e in every if e not in off]
    half = len(off) // 2

    direct = role == 1
    count = {"l_pos": 9 * 16, "ystore": 16, "n_pt": len(off if direct else every), "n_ph": half, "n_pp": len(every) if is_rank else half,
             "n_k0": 2 * len(off if direct else every), "n_k1": 2 * len(off if direct else every), "n_r": 2 * len(on if direct else every),
             "n_x": 2 * (len(off) if is_rank else half), "n_v1": 2 * len(on), "n_v2": 2 * half, "n_v3": 2 * half}
    for n in ("n_ap", "n_at", "n_ah"):
        count[n] = 2 * len(every)
    for n in LOADS:
        count["l_" + n] = 16
    seen = set()

    def need(queue, tag, *events):
        for e in events:
            if (tag, e) not in seen:
                seen.add((tag, e))
                queue.wait_ge(T.sem[e], count.get(e, 1))

    V, S, E = g.vector, g.scalar, g.tensor
    sent = [0]

    def xfer(dst, engines, sem, out, src):
        rid, pid = topo.addr(dst, core)
        sent[0] += len(engines)
        return RemoteDMATransfer(dst_ids=[DstId(rid=rid, pnc=pid)], dma_engine_mask=sum(1 << e for e in engines), remote_sem=T.sem[sem], srcs=[src], dsts=[out])

    def fused(*transfers):
        g.remote_dma_fused(list(transfers), local_sem=T.sem.sent)

    def view(n, name, lo, hi):
        return T[name % n][:, lo:hi].bitcast(dt.uint8) if n == "q" else T[name % n][:, lo:hi]

    def put(n, dst, engines, sem, out, src, lo=0, hi=256):
        return xfer(dst, engines, sem, view(n, out, lo, hi), view(n, src, lo, hi))

    def positions(dst, engines, sem, out, src):
        return xfer(dst, engines, sem, T[out][:, 0:20], T[src][:, 0:20])

    def tile_out(p, dst, key):
        need(g, "g", "q%d" % p)
        for n in "qs":
            fused(put(n, dst, every, "n_a" + key, "b%s_" + key, "a%s" + str(p)))

    def send(what):
        if what in ("k0", "k1"):
            need(g, "g", "q_ky" + what[1])
            lo = 256 * int(what[1])
            for n in "qs":
                fused(put(n, team(twin)[1], off, "n_" + what, "k%s1", "k%s0", lo, lo + 256))
        if what == "r":
            need(g, "g", "q_rt")
            for n in "qs":
                fused(put(n, team(own)[1], on, "n_r", "r%s", "r%s"))
        if what == "x":
            need(g, "g", "q_qx")
            for n in "qs":
                fused(put(n, team(own)[1], on[:half], "n_x", "x%s0", "x%s0"), put(n, team(partner)[2], on[half:], "n_x", "x%s1", "x%s0"),
                      put(n, partner, off, "n_x", "x%s1", "x%s0"))
        if what == "v":
            need(g, "g", "q_vv")
            for n in "qs":
                fused(put(n, twin, off[:half], "n_v2", "v%s2", "v%s0", 0, 128), put(n, diag, off[half:], "n_v3", "v%s3", "v%s0", 0, 128),
                      put(n, partner, on, "n_v1", "v%s1", "v%s0", 0, 128))

    if is_rank:
        g.sync.dma_start(T.pz[:, 0:4], T.kp[:]).then_inc(T.sem["l_pos"], 16)
        for i in range(8):
            (S if i % 2 else g.sync).dma_start(T.pz[16 * i:16 * i + 16, 4:20], T.qp[:]).then_inc(T.sem["l_pos"], 16)
        for n in LOADS:
            out, src = {"ky0": (T.ky_b[:, 0:1024], T.ky[:, 0:1024]), "ky1": (T.ky_b[:, 1024:2048], T.ky[:, 1024:2048]), "rt": (T.rt_b[:], T.rt[:]),
                        "qx": (T.qx_b[:], T.qx[:]), "vv": (T.vv_b[:], T.vv[:])}[n]
            S.dma_start(out, src).then_inc(T.sem["l_" + n], 16)

    def quant(name):
        need(V, "V", "l_" + name)
        q, s, b, lo, n = {"ky0": ("kq0", "ks0", "ky_b", 0, 256), "ky1": ("kq0", "ks0", "ky_b", 256, 256), "qx": ("xq0", "xs0", "qx_b", 0, 256),
                          "rt": ("rq", "rs", "rt_b", 0, 256), "vv": ("vq0", "vs0", "vv_b", 0, 128)}[name]
        V.quantize_mx(T[q][:, lo:lo + n], T[s][:, lo:lo + n], T[b][:, 4 * lo:4 * lo + 4 * n]).then_inc(T.sem["q_" + name], 1)

    KQ, KS = (T.kq0, T.ks0) if is_rank else (T.kq1, T.ks1)
    key_pos = (T.pu, "pu") if is_rank else (T.pt, "n_pt")
    query_pos = ((T.pu, "pu") if is_rank else (T.ph, "n_ph"), (T.pp, "n_pp"))
    query_ready = ("q_qx" if is_rank else "n_x", "n_x")
    rt_ready = "q_rt" if is_rank else "n_r"
    held, turn, bank = {}, {"p": 0, "s": 0}, {}

    def keypos():
        need(V, "V", key_pos[1])
        V.tensor_scalar(T.kf[:], key_pos[0][:, 0:4], 128.0, None, AluOpType.subtract).then_inc(T.sem.kf, 1)

    def offsets(p, b):
        need(V, "V", query_pos[p][1], "kf")
        V.tensor_scalar(T["of%d" % p][:, 16 * b:16 * b + 16], query_pos[p][0][:, 4:20], T.kf[:, b:b + 1], 255.0,
                        AluOpType.subtract, AluOpType.min).then_inc(T.sem["o%d_%d" % (p, b)], 1)

    def product(kind, banks, name, free, b, moving, ready):
        k = banks[turn[kind] % len(banks)]
        turn[kind] += 1
        if k in held:
            need(E, "E", held[k])
        held[k] = free
        bank[name] = T["ps%d" % k]
        need(E, "E", ready, ("q_ky%d" if is_rank else "n_k%d") % (b // 2))
        E.matmul_mx(bank[name][:, 0:256], KQ[:, 128 * b:128 * b + 128], KS[:, 128 * b:128 * b + 128],
                    T[moving % "q"][:, 0:256], T[moving % "s"][:, 0:256], True, True).then_inc(T.sem[name], 1)

    def copy_p(q, b):
        need(V if q == "V" else S, q, "p%d" % b)
        out, src = T.pw[:, 256 * b:256 * b + 256], bank["p%d" % b][:, 0:256]
        i = V.tensor_copy(out, src) if q == "V" else S.activation(out, src, ActivationFunctionType.Copy)
        i.then_inc(T.sem["c%d" % b], 1)

    def pick(q, p, b):
        out = T["u%d" % p][:, 256 * b:256 * b + 256]
        src = T.pw[:, 256 * b:256 * b + 256].indirect(T["of%d" % p][:, 16 * b:16 * b + 16])
        need(V if q == "V" else S, q, "c%d" % b, "o%d_%d" % (p, b))
        i = V.tensor_copy(out, src) if q == "V" else S.activation(out, src, ActivationFunctionType.Copy)
        i.then_inc(T.sem["g%d_%d" % (p, b)], 1)

    def add(p, b):
        need(V, "V", "s%d_%d" % (p, b), "g%d_%d" % (p, b))
        V.tensor_tensor(T["a%d" % p][:, b:1024:4], bank["s%d_%d" % (p, b)][:, 0:256], T["u%d" % p][:, 256 * b:256 * b + 256],
                        AluOpType.add).then_inc(T.sem["d%d_%d" % (p, b)], 1)

    def relu(q, p, b):
        need(V if q == "V" else S, q, "d%d_%d" % (p, b))
        t = T["a%d" % p][:, b:1024:4]
        if q == "V":
            i = V.tensor_scalar(t, t, 0.0, 0.03125, AluOpType.max, AluOpType.mult)
        else:
            i = S.activation(t, t, ActivationFunctionType.Relu, scale=0.03125)
        i.then_inc(T.sem["r%d_%d" % (p, b)], 1)

    def quant_a(p):
        need(V, "V", *["r%d_%d" % (p, b) for b in range(4)])
        V.quantize_mx(T["aq%d" % p][:, 0:256], T["as%d" % p][:, 0:256], T["a%d" % p][:, 0:1024]).then_inc(T.sem["q%d" % p], 1)

    def steps(q, text):
        for w in text.replace("%", str(role - 1)).split():
            k, d = w[0], [int(c) for c in w[1:] if c.isdigit()]
            if w == "kf":
                keypos()
            elif w == "qvv":
                quant("vv")
            elif k == "q":
                quant_a(d[0])
            elif k == "p":
                product("p", (0, 1, 2), "p%d" % d[0], "c%d" % d[0], d[0], "r%s", rt_ready)
            elif k == "s":
                product("s", (3, 4, 5, 6), "s%d_%d" % (d[0], d[1]), "d%d_%d" % (d[0], d[1]), d[1], "x%s" + str(d[0]), query_ready[d[0]])
            elif k == "c":
                copy_p(q, d[0])
            elif k == "g":
                pick(q, d[0], d[1])
            elif k == "o":
                offsets(d[0], d[1])
            elif k == "d":
                add(d[0], d[1])
            elif k == "r":
                relu(q, d[0], d[1])

    if is_rank:
        need(V, "V", "l_pos")
        V.tensor_copy(T.pu[:], T.pz[:]).then_inc(T.sem.pu, 1)
        for n in QUANTS:
            quant(n)
    kind = min(role, 1)
    steps("E", TENSOR[kind])
    steps("V", VECTOR[kind])
    steps("S", SCALAR[kind])

    if role == 1:
        need(g, "g", "n_pt")
        fused(positions(team(own)[2], every, "n_pt", "pt", "pt"))
        need(g, "g", "n_r")
        for n in "qs":
            fused(put(n, team(own)[2], every, "n_r", "r%s", "r%s"))
        for h in range(2):
            need(g, "g", "n_k%d" % h)
            for n in "qs":
                fused(put(n, team(own)[2], every, "n_k%d" % h, "k%s1", "k%s1", 256 * h, 256 * h + 256))
        tile_out(0, own, "t")
    elif role == 2:
        need(g, "g", "n_pp")
        fused(positions(own, every, "n_pp", "pp", "pp"))
        tile_out(1, partner, "h")
    else:
        need(g, "g", "pu")
        fused(positions(team(twin)[1], off, "n_pt", "pt", "pu"), positions(team(own)[1], on[:half], "n_ph", "ph", "pu"),
              positions(team(partner)[2], on[half:], "n_pp", "pp", "pu"))
        for what in SENDS:
            send(what)
        tile_out(1, partner, "p")
        source = {"own": (0, "a%s0", "q_vv", "q0"), "p": (1, "b%s_p", "n_v1", "n_ap"), "t": (2, "b%s_t", "n_v2", "n_at"), "h": (3, "b%s_h", "n_v3", "n_ah")}
        for i, name in enumerate(YORDER):
            v, a, ready, made = source[name]
            need(E, "E", ready, made)
            y = E.matmul_mx(T.ps7[:, 0:256], T["vq%d" % v][:, 0:128], T["vs%d" % v][:, 0:128], T[a % "q"][:, 0:256], T[a % "s"][:, 0:256], i == 0, i == 3)
        y.then_inc(T.sem.ydone, 1)
        need(S, "S", "ydone")
        S.activation(T.yo[:], T.ps7[:, 0:256], ActivationFunctionType.Copy).then_inc(T.sem.ycopy, 1)
        g.sync.wait_ge(T.sem.ycopy, 1)
        g.sync.dma_start(T.y[:], T.yo[:]).then_inc(T.sem.ystore, 16)
        g.sync.wait_ge(T.sem.ystore, 16)
    g.wait_ge(T.sem.sent, sent[0])
